import numpy as np
import ml_dtypes


def mxq(x, axis, fmt="e4m3"):
    dtype, down = {"e4m3": (ml_dtypes.float8_e4m3fn, 7), "e5m2": (ml_dtypes.float8_e5m2, 14)}[fmt]
    v = np.moveaxis(np.asarray(x, np.float32).astype(ml_dtypes.bfloat16).astype(np.float64), axis, -1)
    blocks = v.reshape(v.shape[:-1] + (-1, 32))
    amax = np.abs(blocks).max(-1, keepdims=True)
    byte = np.maximum(np.where(amax > 0, np.frexp(amax)[1] - 1 + 127, 0) - down, 1)
    scale = np.exp2(byte - 127.0)
    codes = (blocks / scale).astype(np.float32).astype(dtype).astype(np.float64)
    return np.moveaxis((codes * scale).reshape(v.shape), -1, axis)


WIDE = False


def mx_kscale(k):
    if not WIDE:
        return np.ones(k)
    levels = np.array([30, -30])
    if k % 512:
        return np.exp2(np.random.permutation(np.resize(levels, k // 32))).repeat(32)
    a = np.empty((k // 512, 16))
    for p in range(k // 512):
        a[p, :8] = np.random.permutation(np.resize(levels, 8))
        for g in range(8):
            far = levels[np.abs(levels - a[p, g]) >= 10]
            a[p, g + 8] = far[np.random.randint(len(far))]
    return np.exp2(a.ravel()).repeat(32)


def f64(x):
    return np.asarray(x).astype(np.float64)


def striped(idx):
    return np.tile(np.asarray(idx).reshape(-1, 16).T, (8, 1)).astype(np.uint16)


def unstriped(offs):
    return offs[:16].T.reshape(-1).astype(np.int64)


def striped8(idx):
    return np.asarray(idx).reshape(8, -1, 16).transpose(0, 2, 1).reshape(128, -1).astype(np.uint16)


def unstriped8(offs):
    return offs.reshape(8, 16, -1).transpose(0, 2, 1).reshape(8, -1).astype(np.int64)


def pick8(x, idx, run):
    r = np.arange(len(x))
    return x[r[:, None], idx[r % (8 * run) // run]]


E2M1 = np.array([0.0, 0.5, 1.0, 1.5, 2.0, 3.0, 4.0, 6.0, -0.0, -0.5, -1.0, -1.5, -2.0, -3.0, -4.0, -6.0])


def pack_weight(w, fmt):
    k, n = w.shape
    w = f64(np.asarray(w, np.float32).astype(ml_dtypes.bfloat16)).reshape(k // 32, 32, n)
    amax = np.abs(w).max(1)
    if fmt in ("e4m3", "e5m2"):
        byte = np.frexp(amax)[1] - 1 + 127 - (7 if fmt == "e4m3" else 14)
    else:
        mant, ex = np.frexp(amax / 6.0)
        byte = np.where(mant > 0.5, ex, ex - 1) + 127
    byte = np.clip(np.where(amax > 0, byte, 1), 1, 254)
    scaled = (w * np.exp2(127.0 - byte)[:, None, :]).reshape(k, n).astype(np.float32)
    by_word = np.ascontiguousarray(scaled.reshape(k // 512, 128, 4, n).transpose(0, 1, 3, 2))
    if fmt in ("e4m3", "e5m2"):
        words = by_word.astype(ml_dtypes.float8_e4m3fn if fmt == "e4m3" else ml_dtypes.float8_e5m2).view(np.uint8)
    else:
        c = by_word.astype(ml_dtypes.float4_e2m1fn).view(np.uint8) & 0xF
        words = (c[..., 0::2] | (c[..., 1::2] << 4)).reshape(k // 512, 128, 2 * n)
    return np.ascontiguousarray(words), np.ascontiguousarray(byte.astype(np.uint8).reshape(k // 512, 16, n))


def unpack_weight(words, scales, fmt):
    g, _, n = scales.shape
    words = np.ascontiguousarray(words).reshape(g, 128, n, -1)
    if fmt in ("e4m3", "e5m2"):
        vals = words.view(ml_dtypes.float8_e4m3fn if fmt == "e4m3" else ml_dtypes.float8_e5m2).astype(np.float64)
    else:
        nib = np.empty((g, 128, n, 4), np.uint8)
        nib[..., 0::2] = words & 0xF
        nib[..., 1::2] = words >> 4
        vals = E2M1[nib]
    vals = vals * np.repeat(np.exp2(scales.astype(np.float64) - 127.0), 8, axis=1)[..., None]
    return vals.transpose(0, 1, 3, 2).reshape(g * 512, n)


K, T, J, R, C, N = 512, 1024, 256, 512, 512, 256


def setup_inputs():
    n = np.random.standard_normal
    idx = np.random.permutation(T)[:J]
    idx2 = np.stack([np.random.permutation(C)[:J] for _ in range(8)])
    idx3 = np.random.permutation(C)[:J]
    idx4 = np.stack([np.random.permutation(C)[:J] for _ in range(8)])
    fk = mx_kscale(K)
    fr = mx_kscale(R)
    xtp = pack_weight(n((K, T)) / fk[:, None], "e2m1")
    wp = pack_weight(n((K, R)) * 1 / np.sqrt(K) * fk[:, None] * fr, "e4m3")
    w2p = pack_weight(n((K, R)) * 1 / np.sqrt(K) * fk[:, None] * fr, "e5m2")
    wbp = pack_weight(n((R, N)) * 1 / np.sqrt(R) / fr[:, None], "e2m1")
    return {
        "xt_words": xtp[0],
        "xt_scales": xtp[1],
        "w_words": wp[0],
        "w_scales": wp[1],
        "w2_words": w2p[0],
        "w2_scales": w2p[1],
        "wb_words": wbp[0],
        "wb_scales": wbp[1],
        "offs": striped(idx),
        "offs2": striped8(idx2),
        "offs3": striped(idx3),
        "offs4": striped8(idx4),
    }


def reference(xt_words, xt_scales, w_words, w_scales, w2_words, w2_scales, wb_words, wb_scales, offs, offs2, offs3, offs4):
    idx = unstriped(offs)
    idx2 = unstriped8(offs2)
    idx3 = unstriped(offs3)
    idx4 = unstriped8(offs4)
    xtu = unpack_weight(xt_words, xt_scales, "e2m1")
    wu = unpack_weight(w_words, w_scales, "e4m3")
    w2u = unpack_weight(w2_words, w2_scales, "e5m2")
    wbu = unpack_weight(wb_words, wb_scales, "e2m1")
    xtidxg = xtu[:, idx]
    a = wu.T @ xtidxg
    b = w2u.T @ xtidxg
    pa = np.zeros((R, C))
    pa[np.arange(R)[:, None], idx2[np.arange(R) % 512 // 64]] = a
    h1 = np.maximum(pa[:, idx3], b)
    pb = np.zeros((R, C))
    pb[np.arange(R)[:, None], idx4[np.arange(R) % 512 // 64]] = h1
    hid = pa + pb
    hidq = mxq(hid, 0, "e5m2")
    p = wbu.T @ hidq
    return p

@@ -1,0 +1,156 @@
+from contextlib import ExitStack
+
+import concourse.mybir as mybir
+
+K, T, J, R, C, N = 512, 1024, 256, 512, 512, 256
+FLOPS = 2 * (2 * K * R * J + R * N * C)
+
+F32 = mybir.dt.float32
+BF16 = mybir.dt.bfloat16
+I32 = mybir.dt.int32
+U32 = mybir.dt.uint32
+U16 = mybir.dt.uint16
+U8 = mybir.dt.uint8
+E4M3 = mybir.dt.float8_e4m3fn_x4
+E5M2 = mybir.dt.float8_e5m2_x4
+E2M1 = mybir.dt.float4_e2m1fn_x4
+COPY = mybir.ActivationFunctionType.Copy
+ADD = mybir.AluOpType.add
+MAX = mybir.AluOpType.max
+
+P = 128
+PACK = 4
+HALF = C // 2
+
+
+def tile_list_writtenagain_kernel(tc, xt_words, xt_scales, w_words, w_scales, w2_words, w2_scales,
+                                      wb_words, wb_scales, offs, offs2, offs3, offs4, out):
+    nc = tc.nc
+    with ExitStack() as ctx:
+        keep = ctx.enter_context(tc.tile_pool(name="keep", bufs=1))
+        psum = ctx.enter_context(tc.psum_pool(name="psum", bufs=1))
+
+        def sb(name, shape, dtype):
+            return keep.tile(shape, dtype, name=name, align_bytes=64)
+
+        def load_list(name, src):
+            lst = keep.tile([P, J // 16], U16, name=name)
+            nc.sync.dma_start(lst[:], src)
+            return lst
+
+        def load_scale_rows(queue, plane, src):
+            for q in range(4):
+                queue.dma_start(plane[32 * q : 32 * q + 4, :].bitcast(I32), src[0, 4 * q : 4 * q + 4, :].bitcast(I32))
+
+        xs_plane = sb("xs_plane", [P, T], U8)
+        ws_raw = sb("ws_raw", [P, R], U8)
+        w2s_raw = sb("w2s_raw", [P, R], U8)
+        wbs_plane = sb("wbs_plane", [P, N], U8)
+        nc.vector.memset(xs_plane[:].bitcast(I32), 0)
+        nc.vector.memset(ws_raw[:].bitcast(I32), 0)
+
+        list1 = load_list("list1", offs)
+        xt_sb = sb("xt_sb", [P, T], U16)
+        nc.sync.dma_start(xt_sb[:].bitcast(I32), xt_words[0].bitcast(I32))
+        load_scale_rows(nc.scalar, xs_plane, xt_scales)
+        w_raw = sb("w_raw", [P, R], U32)
+        nc.sync.dma_start(w_raw[:].bitcast(I32), w_words[0].rearrange("p c t -> p (c t)").bitcast(I32))
+        load_scale_rows(nc.sync, ws_raw, w_scales)
+        list2 = load_list("list2", offs2)
+
+        pa = [sb("pa%d" % t, [P, C], F32) for t in range(PACK)]
+        pb = [sb("pb%d" % t, [P, C], F32) for t in range(PACK)]
+        nc.vector.memset(w2s_raw[:].bitcast(I32), 0)
+        nc.vector.memset(wbs_plane[:].bitcast(I32), 0)
+        for t in range(PACK):
+            nc.vector.memset(pa[t][:], 0.0)
+
+        w2_raw = sb("w2_raw", [P, R], U32)
+        nc.sync.dma_start(w2_raw[:].bitcast(I32), w2_words[0].rearrange("p c t -> p (c t)").bitcast(I32))
+        load_scale_rows(nc.sync, w2s_raw, w2_scales)
+        list3 = load_list("list3", offs3)
+        list4 = load_list("list4", offs4)
+        wb_sb = sb("wb_sb", [P, 2 * N], U8)
+        nc.sync.dma_start(wb_sb[:].bitcast(I32), wb_words[0].bitcast(I32))
+        load_scale_rows(nc.sync, wbs_plane, wb_scales)
+
+        xg_words = sb("xg_words", [P, J], U16)
+        xg_scales = sb("xg_scales", [P, J], U8)
+        nc.vector.tensor_copy(xg_words[:], xt_sb[:].indirect(list1[:]))
+        nc.vector.tensor_copy(xg_scales[:], xs_plane[:].indirect(list1[:]))
+
+        w_dealt = sb("w_dealt", [P, PACK, P], U32)
+        nc.scalar.copy(w_dealt[:].rearrange("p t m -> p m t"), w_raw[:].rearrange("p (m t) -> p m t", t=PACK))
+        ws_first = sb("ws_first", [P, P], U8)
+        ws_rest = sb("ws_rest", [P, PACK - 1, P], U8)
+        ws_by_t = ws_raw[:].rearrange("p (m t) -> p t m", t=PACK)
+        nc.vector.tensor_copy(ws_first[:], ws_by_t[:, 0, :])
+        nc.vector.tensor_copy(ws_rest[:], ws_by_t[:, 1:, :])
+        ws_dealt = [ws_first[:]] + [ws_rest[:, t, :] for t in range(PACK - 1)]
+
+        a_sb = []
+        for t in range(PACK):
+            a_ps = psum.tile([P, J], F32, name="a_ps%d" % t, tag="bank%d" % t)
+            nc.tensor.matmul_mx(a_ps[:], lhsT=w_dealt[:, t, :].bitcast(E4M3), lhsT_scale=ws_dealt[t],
+                                rhs=xg_words[:].bitcast(E2M1), rhs_scale=xg_scales[:], start=True, stop=True)
+            a_t = sb("a_sb%d" % t, [P, J], F32)
+            nc.vector.tensor_copy(a_t[:], a_ps[:])
+            a_sb.append(a_t)
+        for t in range(PACK):
+            nc.scalar.activation(pa[t][:].indirect(list2[:]), a_sb[t][:], COPY)
+
+        w2_dealt = sb("w2_dealt", [P, PACK, P], U32)
+        w2s_dealt = sb("w2s_dealt", [P, PACK, P], U8)
+        nc.vector.tensor_copy(w2_dealt[:].rearrange("p t m -> p m t"), w2_raw[:].rearrange("p (m t) -> p m t", t=PACK))
+        nc.vector.tensor_copy(w2s_dealt[:], w2s_raw[:].rearrange("p (m t) -> p t m", t=PACK))
+        b_ps = [psum.tile([P, 2, J], F32, name="b_ps%d" % u, tag="bank%d" % (PACK + u)) for u in range(2)]
+        for t in range(PACK):
+            nc.tensor.matmul_mx(b_ps[t // 2][:, t % 2, :], lhsT=w2_dealt[:, t, :].bitcast(E5M2), lhsT_scale=w2s_dealt[:, t, :],
+                                rhs=xg_words[:].bitcast(E2M1), rhs_scale=xg_scales[:], start=True, stop=True)
+
+        h1 = []
+        for t in range(PACK):
+            picked = sb("picked%d" % t, [P, J], F32)
+            nc.vector.tensor_copy(picked[:], pa[t][:].indirect(list3[:]))
+            h_t = sb("h1_%d" % t, [P, J], F32)
+            nc.vector.tensor_tensor(h_t[:], b_ps[t // 2][:, t % 2, :], picked[:], MAX)
+            h1.append(h_t)
+        for t in range(PACK):
+            nc.vector.memset(pb[t][:], 0.0)
+        for t in range(PACK):
+            nc.scalar.activation(pb[t][:].indirect(list4[:]), h1[t][:], COPY)
+
+        hid = [sb("hid%d" % u, [P, HALF, PACK], BF16) for u in range(2)]
+        for t in range(PACK):
+            sums = [sb("sum%d_%d" % (t, u), [P, HALF], BF16) for u in range(2)]
+            for u in range(2):
+                cols = slice(u * HALF, (u + 1) * HALF)
+                nc.vector.tensor_tensor(sums[u][:], pa[t][:, cols], pb[t][:, cols], ADD)
+            for u in range(2):
+                nc.vector.tensor_copy(hid[u][:, :, t], sums[u][:])
+
+        codes = [sb("codes%d" % u, [P, HALF], U32) for u in range(2)]
+        scales = [sb("scales%d" % u, [P, HALF], U8) for u in range(2)]
+        for u in range(2):
+            nc.vector.quantize_mx(codes[u][:].bitcast(E5M2), scales[u][:], hid[u][:].rearrange("p c t -> p (c t)"))
+
+        def out_product(dst, u, n):
+            nc.tensor.matmul_mx(dst, lhsT=wb_sb[:, 2 * P * n : 2 * P * (n + 1)].bitcast(E2M1),
+                                lhsT_scale=wbs_plane[:, P * n : P * (n + 1)],
+                                rhs=codes[u][:].bitcast(E5M2), rhs_scale=scales[u][:], start=True, stop=True)
+
+        first_ps = psum.tile([P, 2, HALF], F32, name="first_ps", tag="bank6")
+        for n in range(2):
+            out_product(first_ps[:, n, :], 0, n)
+        first_sb = sb("first_sb", [P, 2, HALF], F32)
+        nc.scalar.copy(first_sb[:], first_ps[:])
+        nc.sync.dma_start(out[:, 0:HALF].rearrange("(n p) c -> p n c", p=P), first_sb[:])
+
+        last_ps = [psum.tile([P, HALF], F32, name="last_ps%d" % n, tag="bank%d" % (7 * (1 - n))) for n in range(2)]
+        last_sb = [sb("last_sb%d" % n, [P, HALF], F32) for n in range(2)]
+        for n in range(2):
+            out_product(last_ps[n][:], 1, n)
+        nc.vector.tensor_copy(last_sb[0][:], last_ps[0][:])
+        nc.sync.dma_start(out[0:P, HALF:C], last_sb[0][:])
+        nc.scalar.copy(last_sb[1][:], last_ps[1][:])
+        nc.scalar.dma_start(out[P : 2 * P, HALF:C], last_sb[1][:])

@@ -20,7 +20,8 @@ MAX = mybir.AluOpType.max
 
 P = 128
 PACK = 4
-HALF = C // 2
+CHUNKS = 4
+WIDTH = C // CHUNKS
 
 
 def tile_list_writtenagain_kernel(tc, xt_words, xt_scales, w_words, w_scales, w2_words, w2_scales,
@@ -30,49 +31,47 @@ def tile_list_writtenagain_kernel(tc, xt_words, xt_scales, w_words, w_scales, w2
         keep = ctx.enter_context(tc.tile_pool(name="keep", bufs=1))
         psum = ctx.enter_context(tc.psum_pool(name="psum", bufs=1))
 
-        def sb(name, shape, dtype):
-            return keep.tile(shape, dtype, name=name, align_bytes=64)
+        def sb(name, shape, dtype, tag=None):
+            return keep.tile(shape, dtype, name=name, tag=tag or name, align_bytes=64)
 
         def load_list(name, src):
             lst = keep.tile([P, J // 16], U16, name=name)
             nc.sync.dma_start(lst[:], src)
             return lst
 
-        def load_scale_rows(queue, plane, src):
-            for q in range(4):
-                queue.dma_start(plane[32 * q : 32 * q + 4, :].bitcast(I32), src[0, 4 * q : 4 * q + 4, :].bitcast(I32))
+        def load_scale_rows(queue, plane, src, quadrants):
+            for q in quadrants:
+                rows = src[0, 4 * q : 4 * q + 4, :].bitcast(I32)
+                queue.dma_start(plane[32 * q : 32 * q + 32, :].bitcast(I32),
+                                rows.unsqueeze(0).to_broadcast([8, 4, src.shape[2] // 4]))
 
         xs_plane = sb("xs_plane", [P, T], U8)
         ws_raw = sb("ws_raw", [P, R], U8)
         w2s_raw = sb("w2s_raw", [P, R], U8)
         wbs_plane = sb("wbs_plane", [P, N], U8)
-        nc.vector.memset(xs_plane[:].bitcast(I32), 0)
-        nc.vector.memset(ws_raw[:].bitcast(I32), 0)
 
         list1 = load_list("list1", offs)
+        load_scale_rows(nc.scalar, xs_plane, xt_scales, range(4))
+        load_scale_rows(nc.sync, ws_raw, w_scales, range(1))
         xt_sb = sb("xt_sb", [P, T], U16)
         nc.sync.dma_start(xt_sb[:].bitcast(I32), xt_words[0].bitcast(I32))
-        load_scale_rows(nc.scalar, xs_plane, xt_scales)
         w_raw = sb("w_raw", [P, R], U32)
         nc.sync.dma_start(w_raw[:].bitcast(I32), w_words[0].rearrange("p c t -> p (c t)").bitcast(I32))
-        load_scale_rows(nc.sync, ws_raw, w_scales)
+        load_scale_rows(nc.sync, ws_raw, w_scales, range(1, 4))
         list2 = load_list("list2", offs2)
 
         pa = [sb("pa%d" % t, [P, C], F32) for t in range(PACK)]
-        pb = [sb("pb%d" % t, [P, C], F32) for t in range(PACK)]
-        nc.vector.memset(w2s_raw[:].bitcast(I32), 0)
-        nc.vector.memset(wbs_plane[:].bitcast(I32), 0)
         for t in range(PACK):
             nc.vector.memset(pa[t][:], 0.0)
 
         w2_raw = sb("w2_raw", [P, R], U32)
         nc.sync.dma_start(w2_raw[:].bitcast(I32), w2_words[0].rearrange("p c t -> p (c t)").bitcast(I32))
-        load_scale_rows(nc.sync, w2s_raw, w2_scales)
+        load_scale_rows(nc.sync, w2s_raw, w2_scales, range(4))
         list3 = load_list("list3", offs3)
         list4 = load_list("list4", offs4)
         wb_sb = sb("wb_sb", [P, 2 * N], U8)
         nc.sync.dma_start(wb_sb[:].bitcast(I32), wb_words[0].bitcast(I32))
-        load_scale_rows(nc.sync, wbs_plane, wb_scales)
+        load_scale_rows(nc.sync, wbs_plane, wb_scales, range(4))
 
         xg_words = sb("xg_words", [P, J], U16)
         xg_scales = sb("xg_scales", [P, J], U8)
@@ -84,8 +83,8 @@ def tile_list_writtenagain_kernel(tc, xt_words, xt_scales, w_words, w_scales, w2
         ws_first = sb("ws_first", [P, P], U8)
         ws_rest = sb("ws_rest", [P, PACK - 1, P], U8)
         ws_by_t = ws_raw[:].rearrange("p (m t) -> p t m", t=PACK)
-        nc.vector.tensor_copy(ws_first[:], ws_by_t[:, 0, :])
-        nc.vector.tensor_copy(ws_rest[:], ws_by_t[:, 1:, :])
+        nc.gpsimd.tensor_copy(ws_first[:], ws_by_t[:, 0, :])
+        nc.gpsimd.tensor_copy(ws_rest[:], ws_by_t[:, 1:, :])
         ws_dealt = [ws_first[:]] + [ws_rest[:, t, :] for t in range(PACK - 1)]
 
         a_sb = []
@@ -101,8 +100,8 @@ def tile_list_writtenagain_kernel(tc, xt_words, xt_scales, w_words, w_scales, w2
 
         w2_dealt = sb("w2_dealt", [P, PACK, P], U32)
         w2s_dealt = sb("w2s_dealt", [P, PACK, P], U8)
-        nc.vector.tensor_copy(w2_dealt[:].rearrange("p t m -> p m t"), w2_raw[:].rearrange("p (m t) -> p m t", t=PACK))
-        nc.vector.tensor_copy(w2s_dealt[:], w2s_raw[:].rearrange("p (m t) -> p t m", t=PACK))
+        nc.gpsimd.tensor_copy(w2_dealt[:], w2_raw[:].rearrange("p (m t) -> p t m", t=PACK))
+        nc.gpsimd.tensor_copy(w2s_dealt[:], w2s_raw[:].rearrange("p (m t) -> p t m", t=PACK))
         b_ps = [psum.tile([P, 2, J], F32, name="b_ps%d" % u, tag="bank%d" % (PACK + u)) for u in range(2)]
         for t in range(PACK):
             nc.tensor.matmul_mx(b_ps[t // 2][:, t % 2, :], lhsT=w2_dealt[:, t, :].bitcast(E5M2), lhsT_scale=w2s_dealt[:, t, :],
@@ -110,47 +109,49 @@ def tile_list_writtenagain_kernel(tc, xt_words, xt_scales, w_words, w_scales, w2
 
         h1 = []
         for t in range(PACK):
-            picked = sb("picked%d" % t, [P, J], F32)
+            picked = sb("picked%d" % t, [P, J], F32, tag="picked")
             nc.vector.tensor_copy(picked[:], pa[t][:].indirect(list3[:]))
             h_t = sb("h1_%d" % t, [P, J], F32)
             nc.vector.tensor_tensor(h_t[:], b_ps[t // 2][:, t % 2, :], picked[:], MAX)
             h1.append(h_t)
+        pb = [sb("pb%d" % t, [P, C], F32, tag=tag) for t, tag in enumerate(("ws_raw", "w2_raw", "w2s_raw", "w_dealt"))]
         for t in range(PACK):
-            nc.vector.memset(pb[t][:], 0.0)
+            nc.gpsimd.memset(pb[t][:], 0.0)
         for t in range(PACK):
             nc.scalar.activation(pb[t][:].indirect(list4[:]), h1[t][:], COPY)
 
-        hid = [sb("hid%d" % u, [P, HALF, PACK], BF16) for u in range(2)]
-        for t in range(PACK):
-            sums = [sb("sum%d_%d" % (t, u), [P, HALF], BF16) for u in range(2)]
-            for u in range(2):
-                cols = slice(u * HALF, (u + 1) * HALF)
-                nc.vector.tensor_tensor(sums[u][:], pa[t][:, cols], pb[t][:, cols], ADD)
-            for u in range(2):
-                nc.vector.tensor_copy(hid[u][:, :, t], sums[u][:])
+        hid = [sb("hid%d" % u, [P, WIDTH, PACK], BF16) for u in range(CHUNKS)]
+        cols = [slice(u * WIDTH, (u + 1) * WIDTH) for u in range(CHUNKS)]
+        sums01 = sb("sums01", [P, 2, C], BF16)
+        for t in range(2):
+            nc.vector.tensor_tensor(sums01[:, t, :], pa[t][:], pb[t][:], ADD)
+        for u in range(CHUNKS):
+            nc.vector.tensor_copy(hid[u][:, :, 0:2], sums01[:, :, cols[u]].rearrange("p e c -> p c e"))
+        sums23 = [sb("sums23_%d" % u, [P, 2, WIDTH], BF16) for u in range(CHUNKS)]
+        for u in range(CHUNKS):
+            nc.vector.tensor_tensor(sums23[u][:, 0, :], pa[2][:, cols[u]], pb[2][:, cols[u]], ADD)
 
-        codes = [sb("codes%d" % u, [P, HALF], U32) for u in range(2)]
-        scales = [sb("scales%d" % u, [P, HALF], U8) for u in range(2)]
-        for u in range(2):
-            nc.vector.quantize_mx(codes[u][:].bitcast(E5M2), scales[u][:], hid[u][:].rearrange("p c t -> p (c t)"))
+        codes = [sb("codes%d" % u, [P, WIDTH], U32) for u in range(CHUNKS)]
+        scales = [sb("scales%d" % u, [P, WIDTH], U8) for u in range(CHUNKS)]
+        for first in range(0, CHUNKS, 2):
+            both = (first, first + 1)
+            for u in both:
+                nc.vector.tensor_tensor(sums23[u][:, 1, :], pa[3][:, cols[u]], pb[3][:, cols[u]], ADD)
+            for u in both:
+                nc.vector.tensor_copy(hid[u][:, :, 2:4], sums23[u][:].rearrange("p e c -> p c e"))
+            for u in both:
+                nc.vector.quantize_mx(codes[u][:].bitcast(E5M2), scales[u][:], hid[u][:].rearrange("p c t -> p (c t)"))
 
-        def out_product(dst, u, n):
-            nc.tensor.matmul_mx(dst, lhsT=wb_sb[:, 2 * P * n : 2 * P * (n + 1)].bitcast(E2M1),
-                                lhsT_scale=wbs_plane[:, P * n : P * (n + 1)],
-                                rhs=codes[u][:].bitcast(E5M2), rhs_scale=scales[u][:], start=True, stop=True)
-
-        first_ps = psum.tile([P, 2, HALF], F32, name="first_ps", tag="bank6")
-        for n in range(2):
-            out_product(first_ps[:, n, :], 0, n)
-        first_sb = sb("first_sb", [P, 2, HALF], F32)
-        nc.scalar.copy(first_sb[:], first_ps[:])
-        nc.sync.dma_start(out[:, 0:HALF].rearrange("(n p) c -> p n c", p=P), first_sb[:])
-
-        last_ps = [psum.tile([P, HALF], F32, name="last_ps%d" % n, tag="bank%d" % (7 * (1 - n))) for n in range(2)]
-        last_sb = [sb("last_sb%d" % n, [P, HALF], F32) for n in range(2)]
-        for n in range(2):
-            out_product(last_ps[n][:], 1, n)
-        nc.vector.tensor_copy(last_sb[0][:], last_ps[0][:])
-        nc.sync.dma_start(out[0:P, HALF:C], last_sb[0][:])
-        nc.scalar.copy(last_sb[1][:], last_ps[1][:])
-        nc.scalar.dma_start(out[P : 2 * P, HALF:C], last_sb[1][:])
+        for u in range(CHUNKS):
+            out_ps = psum.tile([P, 2, WIDTH], F32, name="out_ps%d" % u, tag="bank%d" % u)
+            for n in range(2):
+                nc.tensor.matmul_mx(out_ps[:, n, :], lhsT=wb_sb[:, 2 * P * n : 2 * P * (n + 1)].bitcast(E2M1),
+                                    lhsT_scale=wbs_plane[:, P * n : P * (n + 1)],
+                                    rhs=codes[u][:].bitcast(E5M2), rhs_scale=scales[u][:], start=True, stop=True)
+            out_sb = sb("out_sb%d" % u, [P, 2, WIDTH], F32)
+            if u < CHUNKS - 1:
+                nc.scalar.copy(out_sb[:], out_ps[:])
+            else:
+                nc.vector.tensor_copy(out_sb[:], out_ps[:])
+            queue = nc.scalar if u == CHUNKS - 2 else nc.sync
+            queue.dma_start(out[:, cols[u]].rearrange("(n p) c -> p n c", p=P), out_sb[:])

@@ -39,39 +39,42 @@ def tile_list_writtenagain_kernel(tc, xt_words, xt_scales, w_words, w_scales, w2
             nc.sync.dma_start(lst[:], src)
             return lst
 
-        def load_scale_rows(queue, plane, src, quadrants):
-            for q in quadrants:
-                rows = src[0, 4 * q : 4 * q + 4, :].bitcast(I32)
-                queue.dma_start(plane[32 * q : 32 * q + 32, :].bitcast(I32),
-                                rows.unsqueeze(0).to_broadcast([8, 4, src.shape[2] // 4]))
+        def load_scale_rows(queue, plane, src):
+            for q in range(4):
+                queue.dma_start(plane[32 * q : 32 * q + 4, :].bitcast(I32), src[0, 4 * q : 4 * q + 4, :].bitcast(I32))
 
         xs_plane = sb("xs_plane", [P, T], U8)
-        ws_raw = sb("ws_raw", [P, R], U8)
+        ws_raw = sb("ws_raw", [P, 2, R], U8)
         w2s_raw = sb("w2s_raw", [P, R], U8)
         wbs_plane = sb("wbs_plane", [P, N], U8)
+        nc.vector.memset(xs_plane[:].bitcast(I32), 0)
+        nc.vector.memset(ws_raw[:].rearrange("p h n -> p (h n)").bitcast(I32), 0)
 
         list1 = load_list("list1", offs)
-        load_scale_rows(nc.scalar, xs_plane, xt_scales, range(4))
-        load_scale_rows(nc.sync, ws_raw, w_scales, range(1))
         xt_sb = sb("xt_sb", [P, T], U16)
         nc.sync.dma_start(xt_sb[:].bitcast(I32), xt_words[0].bitcast(I32))
+        load_scale_rows(nc.scalar, xs_plane, xt_scales)
         w_raw = sb("w_raw", [P, R], U32)
         nc.sync.dma_start(w_raw[:].bitcast(I32), w_words[0].rearrange("p c t -> p (c t)").bitcast(I32))
-        load_scale_rows(nc.sync, ws_raw, w_scales, range(1, 4))
+        ws_rows = w_scales[0].bitcast(I32).rearrange("(h q r) n -> q r h n", h=2, q=2)
+        for q in range(2):
+            nc.sync.dma_start(ws_raw[32 * q : 32 * q + 4, :, :].bitcast(I32), ws_rows[q])
         list2 = load_list("list2", offs2)
 
         pa = [sb("pa%d" % t, [P, C], F32) for t in range(PACK)]
+        nc.vector.memset(w2s_raw[:].bitcast(I32), 0)
+        nc.vector.memset(wbs_plane[:].bitcast(I32), 0)
         for t in range(PACK):
             nc.vector.memset(pa[t][:], 0.0)
 
         w2_raw = sb("w2_raw", [P, R], U32)
         nc.sync.dma_start(w2_raw[:].bitcast(I32), w2_words[0].rearrange("p c t -> p (c t)").bitcast(I32))
-        load_scale_rows(nc.sync, w2s_raw, w2_scales, range(4))
+        load_scale_rows(nc.sync, w2s_raw, w2_scales)
         list3 = load_list("list3", offs3)
         list4 = load_list("list4", offs4)
         wb_sb = sb("wb_sb", [P, 2 * N], U8)
         nc.sync.dma_start(wb_sb[:].bitcast(I32), wb_words[0].bitcast(I32))
-        load_scale_rows(nc.sync, wbs_plane, wb_scales, range(4))
+        load_scale_rows(nc.sync, wbs_plane, wb_scales)
 
         xg_words = sb("xg_words", [P, J], U16)
         xg_scales = sb("xg_scales", [P, J], U8)
@@ -80,29 +83,27 @@ def tile_list_writtenagain_kernel(tc, xt_words, xt_scales, w_words, w_scales, w2
 
         w_dealt = sb("w_dealt", [P, PACK, P], U32)
         nc.scalar.copy(w_dealt[:].rearrange("p t m -> p m t"), w_raw[:].rearrange("p (m t) -> p m t", t=PACK))
-        ws_first = sb("ws_first", [P, P], U8)
-        ws_rest = sb("ws_rest", [P, PACK - 1, P], U8)
-        ws_by_t = ws_raw[:].rearrange("p (m t) -> p t m", t=PACK)
-        nc.gpsimd.tensor_copy(ws_first[:], ws_by_t[:, 0, :])
-        nc.gpsimd.tensor_copy(ws_rest[:], ws_by_t[:, 1:, :])
-        ws_dealt = [ws_first[:]] + [ws_rest[:, t, :] for t in range(PACK - 1)]
+        ws_dealt = sb("ws_dealt", [P, 2, PACK * P], U8, tag="xt_sb")
+        nc.vector.tensor_copy(ws_dealt[:].rearrange("p h (t m) -> p h t m", t=PACK), ws_raw[:].rearrange("p h (m t) -> p h t m", t=PACK))
+        nc.vector.tensor_copy(ws_dealt[64:128, 0, :].bitcast(I32), ws_dealt[0:64, 1, :].bitcast(I32))
 
+        pieces = [(0, 0, J // 2), (0, J // 2, J)] + [(t, 0, J) for t in range(1, PACK)]
         a_sb = []
-        for t in range(PACK):
-            a_ps = psum.tile([P, J], F32, name="a_ps%d" % t, tag="bank%d" % t)
-            nc.tensor.matmul_mx(a_ps[:], lhsT=w_dealt[:, t, :].bitcast(E4M3), lhsT_scale=ws_dealt[t],
-                                rhs=xg_words[:].bitcast(E2M1), rhs_scale=xg_scales[:], start=True, stop=True)
-            a_t = sb("a_sb%d" % t, [P, J], F32)
-            nc.vector.tensor_copy(a_t[:], a_ps[:])
-            a_sb.append(a_t)
-        for t in range(PACK):
-            nc.scalar.activation(pa[t][:].indirect(list2[:]), a_sb[t][:], COPY)
+        for i, (t, lo, hi) in enumerate(pieces):
+            a_ps = psum.tile([P, hi - lo], F32, name="a_ps%d" % i, tag="bank%d" % i)
+            nc.tensor.matmul_mx(a_ps[:], lhsT=w_dealt[:, t, :].bitcast(E4M3), lhsT_scale=ws_dealt[:, 0, t * P : (t + 1) * P],
+                                rhs=xg_words[:, lo:hi].bitcast(E2M1), rhs_scale=xg_scales[:, lo:hi], start=True, stop=True)
+            a_piece = sb("a_sb%d" % i, [P, hi - lo], F32)
+            nc.vector.tensor_copy(a_piece[:], a_ps[:])
+            a_sb.append(a_piece)
+        for i, (t, lo, hi) in enumerate(pieces):
+            nc.scalar.activation(pa[t][:].indirect(list2[:, lo // 16 : hi // 16]), a_sb[i][:], COPY)
 
         w2_dealt = sb("w2_dealt", [P, PACK, P], U32)
         w2s_dealt = sb("w2s_dealt", [P, PACK, P], U8)
-        nc.gpsimd.tensor_copy(w2_dealt[:], w2_raw[:].rearrange("p (m t) -> p t m", t=PACK))
-        nc.gpsimd.tensor_copy(w2s_dealt[:], w2s_raw[:].rearrange("p (m t) -> p t m", t=PACK))
-        b_ps = [psum.tile([P, 2, J], F32, name="b_ps%d" % u, tag="bank%d" % (PACK + u)) for u in range(2)]
+        nc.vector.tensor_copy(w2_dealt[:].rearrange("p t m -> p m t"), w2_raw[:].rearrange("p (m t) -> p m t", t=PACK))
+        nc.vector.tensor_copy(w2s_dealt[:], w2s_raw[:].rearrange("p (m t) -> p t m", t=PACK))
+        b_ps = [psum.tile([P, 2, J], F32, name="b_ps%d" % u, tag="bank%d" % (len(pieces) + u)) for u in range(2)]
         for t in range(PACK):
             nc.tensor.matmul_mx(b_ps[t // 2][:, t % 2, :], lhsT=w2_dealt[:, t, :].bitcast(E5M2), lhsT_scale=w2s_dealt[:, t, :],
                                 rhs=xg_words[:].bitcast(E2M1), rhs_scale=xg_scales[:], start=True, stop=True)
@@ -114,44 +115,65 @@ def tile_list_writtenagain_kernel(tc, xt_words, xt_scales, w_words, w_scales, w2
             h_t = sb("h1_%d" % t, [P, J], F32)
             nc.vector.tensor_tensor(h_t[:], b_ps[t // 2][:, t % 2, :], picked[:], MAX)
             h1.append(h_t)
-        pb = [sb("pb%d" % t, [P, C], F32, tag=tag) for t, tag in enumerate(("ws_raw", "w2_raw", "w2s_raw", "w_dealt"))]
+        pb = [sb("pb%d" % t, [P, C], F32, tag=tag) for t, tag in enumerate(("w_dealt", "w2_raw", "w2s_raw", "w2_dealt"))]
         for t in range(PACK):
-            nc.gpsimd.memset(pb[t][:], 0.0)
+            nc.vector.memset(pb[t][:], 0.0)
         for t in range(PACK):
             nc.scalar.activation(pb[t][:].indirect(list4[:]), h1[t][:], COPY)
 
         hid = [sb("hid%d" % u, [P, WIDTH, PACK], BF16) for u in range(CHUNKS)]
         cols = [slice(u * WIDTH, (u + 1) * WIDTH) for u in range(CHUNKS)]
-        sums01 = sb("sums01", [P, 2, C], BF16)
+        sums = sb("sums", [P, CHUNKS, PACK, WIDTH], BF16, tag="picked")
+
+        def by_chunk(board):
+            return board[:].rearrange("p (u c) -> p u c", u=CHUNKS)
+
+        def weave(copy, u, pair):
+            copy(hid[u][:, :, 2 * pair : 2 * pair + 2], sums[:, u, 2 * pair : 2 * pair + 2, :].rearrange("p e c -> p c e"))
+
         for t in range(2):
-            nc.vector.tensor_tensor(sums01[:, t, :], pa[t][:], pb[t][:], ADD)
+            nc.vector.tensor_tensor(sums[:, :, t, :], by_chunk(pa[t]), by_chunk(pb[t]), ADD)
         for u in range(CHUNKS):
-            nc.vector.tensor_copy(hid[u][:, :, 0:2], sums01[:, :, cols[u]].rearrange("p e c -> p c e"))
-        sums23 = [sb("sums23_%d" % u, [P, 2, WIDTH], BF16) for u in range(CHUNKS)]
-        for u in range(CHUNKS):
-            nc.vector.tensor_tensor(sums23[u][:, 0, :], pa[2][:, cols[u]], pb[2][:, cols[u]], ADD)
+            weave(nc.vector.tensor_copy, u, 0)
+        nc.vector.tensor_tensor(sums[:, :, 2, :], by_chunk(pa[2]), by_chunk(pb[2]), ADD)
 
         codes = [sb("codes%d" % u, [P, WIDTH], U32) for u in range(CHUNKS)]
         scales = [sb("scales%d" % u, [P, WIDTH], U8) for u in range(CHUNKS)]
-        for first in range(0, CHUNKS, 2):
-            both = (first, first + 1)
-            for u in both:
-                nc.vector.tensor_tensor(sums23[u][:, 1, :], pa[3][:, cols[u]], pb[3][:, cols[u]], ADD)
-            for u in both:
-                nc.vector.tensor_copy(hid[u][:, :, 2:4], sums23[u][:].rearrange("p e c -> p c e"))
-            for u in both:
-                nc.vector.quantize_mx(codes[u][:].bitcast(E5M2), scales[u][:], hid[u][:].rearrange("p c t -> p (c t)"))
 
-        for u in range(CHUNKS):
+        def add_last(u):
+            nc.vector.tensor_tensor(sums[:, u, 3, :], pa[3][:, cols[u]], pb[3][:, cols[u]], ADD)
+
+        def quantise(u):
+            nc.vector.quantize_mx(codes[u][:].bitcast(E5M2), scales[u][:], hid[u][:].rearrange("p c t -> p (c t)"))
+
+        add_last(0)
+        for u in (1, 3):
+            add_last(u)
+            weave(nc.scalar.copy, u, 1)
+        weave(nc.vector.tensor_copy, 0, 1)
+        add_last(2)
+        quantise(0)
+        weave(nc.vector.tensor_copy, 2, 1)
+        for u in range(1, CHUNKS):
+            quantise(u)
+
+        def out_product(dst, u, n):
+            nc.tensor.matmul_mx(dst, lhsT=wb_sb[:, 2 * P * n : 2 * P * (n + 1)].bitcast(E2M1),
+                                lhsT_scale=wbs_plane[:, P * n : P * (n + 1)],
+                                rhs=codes[u][:].bitcast(E5M2), rhs_scale=scales[u][:], start=True, stop=True)
+
+        copies = (nc.scalar.copy, nc.vector.tensor_copy)
+        for u in range(CHUNKS - 1):
             out_ps = psum.tile([P, 2, WIDTH], F32, name="out_ps%d" % u, tag="bank%d" % u)
             for n in range(2):
-                nc.tensor.matmul_mx(out_ps[:, n, :], lhsT=wb_sb[:, 2 * P * n : 2 * P * (n + 1)].bitcast(E2M1),
-                                    lhsT_scale=wbs_plane[:, P * n : P * (n + 1)],
-                                    rhs=codes[u][:].bitcast(E5M2), rhs_scale=scales[u][:], start=True, stop=True)
+                out_product(out_ps[:, n, :], u, n)
             out_sb = sb("out_sb%d" % u, [P, 2, WIDTH], F32)
-            if u < CHUNKS - 1:
-                nc.scalar.copy(out_sb[:], out_ps[:])
-            else:
-                nc.vector.tensor_copy(out_sb[:], out_ps[:])
-            queue = nc.scalar if u == CHUNKS - 2 else nc.sync
-            queue.dma_start(out[:, cols[u]].rearrange("(n p) c -> p n c", p=P), out_sb[:])
+            copies[u % 2](out_sb[:], out_ps[:])
+            nc.sync.dma_start(out[:, cols[u]].rearrange("(n p) c -> p n c", p=P), out_sb[:])
+        last = CHUNKS - 1
+        for n, queue in enumerate((nc.sync, nc.scalar)):
+            last_ps = psum.tile([P, WIDTH], F32, name="last_ps%d" % n, tag="bank%d" % (last + n))
+            out_product(last_ps[:], last, n)
+            last_sb = sb("last_sb%d" % n, [P, WIDTH], F32)
+            copies[1 - n](last_sb[:], last_ps[:])
+            queue.dma_start(out[P * n : P * (n + 1), cols[last]], last_sb[:])

@@ -45,7 +45,7 @@ def tile_list_writtenagain_kernel(tc, xt_words, xt_scales, w_words, w_scales, w2
 
         xs_plane = sb("xs_plane", [P, T], U8)
         ws_raw = sb("ws_raw", [P, 2, R], U8)
-        w2s_raw = sb("w2s_raw", [P, R], U8)
+        w2s_raw = sb("w2s_raw", [P, R], U8, tag="picked")
         wbs_plane = sb("wbs_plane", [P, N], U8)
         nc.vector.memset(xs_plane[:].bitcast(I32), 0)
         nc.vector.memset(ws_raw[:].rearrange("p h n -> p (h n)").bitcast(I32), 0)
@@ -76,37 +76,63 @@ def tile_list_writtenagain_kernel(tc, xt_words, xt_scales, w_words, w_scales, w2
         nc.sync.dma_start(wb_sb[:].bitcast(I32), wb_words[0].bitcast(I32))
         load_scale_rows(nc.sync, wbs_plane, wb_scales)
 
-        xg_words = sb("xg_words", [P, J], U16)
-        xg_scales = sb("xg_scales", [P, J], U8)
-        nc.vector.tensor_copy(xg_words[:], xt_sb[:].indirect(list1[:]))
-        nc.vector.tensor_copy(xg_scales[:], xs_plane[:].indirect(list1[:]))
+        halves = [slice(0, J // 2), slice(J // 2, J)]
+        entries = [list1[:, 0 : J // 32], list1[:, J // 32 : J // 16]]
+        xgs_first = sb("xgs_first", [P, J // 2], U8)
+        xg_first = sb("xg_first", [P, J // 2], U16)
+        nc.vector.tensor_copy(xg_first[:], xt_sb[:].indirect(entries[0]))
+        nc.vector.tensor_copy(xgs_first[:], xs_plane[:].indirect(entries[0]))
 
         w_dealt = sb("w_dealt", [P, PACK, P], U32)
-        nc.scalar.copy(w_dealt[:].rearrange("p t m -> p m t"), w_raw[:].rearrange("p (m t) -> p m t", t=PACK))
-        ws_dealt = sb("ws_dealt", [P, 2, PACK * P], U8, tag="xt_sb")
-        nc.vector.tensor_copy(ws_dealt[:].rearrange("p h (t m) -> p h t m", t=PACK), ws_raw[:].rearrange("p h (m t) -> p h t m", t=PACK))
-        nc.vector.tensor_copy(ws_dealt[64:128, 0, :].bitcast(I32), ws_dealt[0:64, 1, :].bitcast(I32))
+        w_by_slice = w_raw[:].rearrange("p (m t) -> p t m", t=PACK)
+        nc.scalar.copy(w_dealt[:, 0, :], w_by_slice[:, 0, :])
+        nc.scalar.copy(w_dealt[:, 1:, :], w_by_slice[:, 1:, :])
 
-        pieces = [(0, 0, J // 2), (0, J // 2, J)] + [(t, 0, J) for t in range(1, PACK)]
-        a_sb = []
-        for i, (t, lo, hi) in enumerate(pieces):
-            a_ps = psum.tile([P, hi - lo], F32, name="a_ps%d" % i, tag="bank%d" % i)
-            nc.tensor.matmul_mx(a_ps[:], lhsT=w_dealt[:, t, :].bitcast(E4M3), lhsT_scale=ws_dealt[:, 0, t * P : (t + 1) * P],
-                                rhs=xg_words[:, lo:hi].bitcast(E2M1), rhs_scale=xg_scales[:, lo:hi], start=True, stop=True)
-            a_piece = sb("a_sb%d" % i, [P, hi - lo], F32)
-            nc.vector.tensor_copy(a_piece[:], a_ps[:])
-            a_sb.append(a_piece)
-        for i, (t, lo, hi) in enumerate(pieces):
-            nc.scalar.activation(pa[t][:].indirect(list2[:, lo // 16 : hi // 16]), a_sb[i][:], COPY)
+        ws_by_slice = ws_raw[:].rearrange("p h (m t) -> p h t m", t=PACK)
+        ws_upper = sb("ws_upper", [P, 2, P], U8)
+        ws01 = sb("ws01", [P, 2, P], U8)
+        nc.vector.tensor_copy(ws_upper[:], ws_by_slice[:, 1, 0:2, :])
+        nc.vector.tensor_copy(ws01[:], ws_by_slice[:, 0, 0:2, :])
+        nc.vector.tensor_copy(ws01[64:128].rearrange("p t m -> p (t m)").bitcast(I32),
+                              ws_upper[0:64].rearrange("p t m -> p (t m)").bitcast(I32))
+        xg_second = sb("xg_second", [P, J // 2], U16, tag="ws_upper")
+        nc.vector.tensor_copy(xg_second[:], xt_sb[:].indirect(entries[1]))
+        xgs_second = sb("xgs_second", [P, J // 2], U8, tag="xt_sb")
+        nc.vector.tensor_copy(xgs_second[:], xs_plane[:].indirect(entries[1]))
+        xg_words = [xg_first, xg_second]
+        xg_scales = [xgs_first, xgs_second]
 
-        w2_dealt = sb("w2_dealt", [P, PACK, P], U32)
-        w2s_dealt = sb("w2s_dealt", [P, PACK, P], U8)
+        def slot_product(dst, words, fmt, plane, g):
+            nc.tensor.matmul_mx(dst, lhsT=words.bitcast(fmt), lhsT_scale=plane, rhs=xg_words[g][:].bitcast(E2M1),
+                                rhs_scale=xg_scales[g][:], start=True, stop=True)
+
+        def first_results(t, plane, groups, bank):
+            a_ps = psum.tile([P, len(groups), J // 2], F32, name="a_ps%d" % bank, tag="bank%d" % bank)
+            for i, g in enumerate(groups):
+                slot_product(a_ps[:, i, :], w_dealt[:, t, :], E4M3, plane, g)
+            a_sb = sb("a_sb%d" % bank, [P, len(groups) * J // 2], F32)
+            copy = nc.scalar.copy if bank == 0 else nc.vector.tensor_copy
+            copy(a_sb[:], a_ps[:].rearrange("p g j -> p (g j)"))
+            columns = slice(groups[0] * J // 32, (groups[-1] + 1) * J // 32)
+            nc.scalar.activation(pa[t][:].indirect(list2[:, columns]), a_sb[:], COPY)
+
+        for g in range(2):
+            for t in range(2):
+                first_results(t, ws01[:, t, :], [g], 2 * g + t)
+        ws23 = sb("ws23", [P, 2, 2 * P], U8, tag="xs_plane")
+        nc.vector.tensor_copy(ws23[:].rearrange("p h (t m) -> p h t m", t=2), ws_by_slice[:, :, 2:4, :])
+        nc.vector.tensor_copy(ws23[64:128, 0, :].bitcast(I32), ws23[0:64, 1, :].bitcast(I32))
+        first_results(2, ws23[:, 0, 0:P], [0, 1], 4)
+        first_results(3, ws23[:, 0, P : 2 * P], [0, 1], 5)
+
+        w2_dealt = sb("w2_dealt", [P, PACK, P], U32, tag="ws01")
+        w2s_dealt = sb("w2s_dealt", [P, PACK, P], U8, tag="ws_raw")
         nc.vector.tensor_copy(w2_dealt[:].rearrange("p t m -> p m t"), w2_raw[:].rearrange("p (m t) -> p m t", t=PACK))
         nc.vector.tensor_copy(w2s_dealt[:], w2s_raw[:].rearrange("p (m t) -> p t m", t=PACK))
-        b_ps = [psum.tile([P, 2, J], F32, name="b_ps%d" % u, tag="bank%d" % (len(pieces) + u)) for u in range(2)]
+        b_ps = [psum.tile([P, 2, J], F32, name="b_ps%d" % u, tag="bank%d" % (6 + u)) for u in range(2)]
         for t in range(PACK):
-            nc.tensor.matmul_mx(b_ps[t // 2][:, t % 2, :], lhsT=w2_dealt[:, t, :].bitcast(E5M2), lhsT_scale=w2s_dealt[:, t, :],
-                                rhs=xg_words[:].bitcast(E2M1), rhs_scale=xg_scales[:], start=True, stop=True)
+            for g in range(2):
+                slot_product(b_ps[t // 2][:, t % 2, halves[g]], w2_dealt[:, t, :], E5M2, w2s_dealt[:, t, :], g)
 
         h1 = []
         for t in range(PACK):
@@ -115,7 +141,7 @@ def tile_list_writtenagain_kernel(tc, xt_words, xt_scales, w_words, w_scales, w2
             h_t = sb("h1_%d" % t, [P, J], F32)
             nc.vector.tensor_tensor(h_t[:], b_ps[t // 2][:, t % 2, :], picked[:], MAX)
             h1.append(h_t)
-        pb = [sb("pb%d" % t, [P, C], F32, tag=tag) for t, tag in enumerate(("w_dealt", "w2_raw", "w2s_raw", "w2_dealt"))]
+        pb = [sb("pb%d" % t, [P, C], F32, tag=tag) for t, tag in enumerate(("w2_raw", "xgs_first", "xg_first", "ws_upper"))]
         for t in range(PACK):
             nc.vector.memset(pb[t][:], 0.0)
         for t in range(PACK):

from contextlib import ExitStack

import concourse.mybir as mybir

K, T, J, R, C, N = 512, 1024, 256, 512, 512, 256
FLOPS = 2 * (2 * K * R * J + R * N * C)

F32 = mybir.dt.float32
BF16 = mybir.dt.bfloat16
I32 = mybir.dt.int32
U32 = mybir.dt.uint32
U16 = mybir.dt.uint16
U8 = mybir.dt.uint8
E4M3 = mybir.dt.float8_e4m3fn_x4
E5M2 = mybir.dt.float8_e5m2_x4
E2M1 = mybir.dt.float4_e2m1fn_x4
COPY = mybir.ActivationFunctionType.Copy
ADD = mybir.AluOpType.add
MAX = mybir.AluOpType.max

P = 128
PACK = 4
CHUNKS = 4
WIDTH = C // CHUNKS


def tile_list_writtenagain_kernel(tc, xt_words, xt_scales, w_words, w_scales, w2_words, w2_scales,
                                      wb_words, wb_scales, offs, offs2, offs3, offs4, out):
    nc = tc.nc
    with ExitStack() as ctx:
        keep = ctx.enter_context(tc.tile_pool(name="keep", bufs=1))
        psum = ctx.enter_context(tc.psum_pool(name="psum", bufs=1))

        def sb(name, shape, dtype, tag=None):
            return keep.tile(shape, dtype, name=name, tag=tag or name, align_bytes=64)

        def load_list(name, src):
            lst = keep.tile([P, J // 16], U16, name=name)
            nc.sync.dma_start(lst[:], src)
            return lst

        def load_scale_rows(queue, plane, src):
            for q in range(4):
                queue.dma_start(plane[32 * q : 32 * q + 4, :].bitcast(I32), src[0, 4 * q : 4 * q + 4, :].bitcast(I32))

        xs_plane = sb("xs_plane", [P, T], U8)
        ws_raw = sb("ws_raw", [P, 2, R], U8)
        w2s_raw = sb("w2s_raw", [P, R], U8, tag="picked")
        wbs_plane = sb("wbs_plane", [P, N], U8)
        nc.vector.memset(xs_plane[:].bitcast(I32), 0)
        nc.vector.memset(ws_raw[:].rearrange("p h n -> p (h n)").bitcast(I32), 0)

        list1 = load_list("list1", offs)
        xt_sb = sb("xt_sb", [P, T], U16)
        nc.sync.dma_start(xt_sb[:].bitcast(I32), xt_words[0].bitcast(I32))
        load_scale_rows(nc.scalar, xs_plane, xt_scales)
        w_raw = sb("w_raw", [P, R], U32)
        nc.sync.dma_start(w_raw[:].bitcast(I32), w_words[0].rearrange("p c t -> p (c t)").bitcast(I32))
        ws_rows = w_scales[0].bitcast(I32).rearrange("(h q r) n -> q r h n", h=2, q=2)
        for q in range(2):
            nc.sync.dma_start(ws_raw[32 * q : 32 * q + 4, :, :].bitcast(I32), ws_rows[q])
        list2 = load_list("list2", offs2)

        pa = [sb("pa%d" % t, [P, C], F32) for t in range(PACK)]
        nc.vector.memset(w2s_raw[:].bitcast(I32), 0)
        nc.vector.memset(wbs_plane[:].bitcast(I32), 0)
        for t in range(PACK):
            nc.vector.memset(pa[t][:], 0.0)

        w2_raw = sb("w2_raw", [P, R], U32)
        nc.sync.dma_start(w2_raw[:].bitcast(I32), w2_words[0].rearrange("p c t -> p (c t)").bitcast(I32))
        load_scale_rows(nc.sync, w2s_raw, w2_scales)
        list3 = load_list("list3", offs3)
        list4 = load_list("list4", offs4)
        wb_sb = sb("wb_sb", [P, 2 * N], U8)
        nc.sync.dma_start(wb_sb[:].bitcast(I32), wb_words[0].bitcast(I32))
        load_scale_rows(nc.sync, wbs_plane, wb_scales)

        halves = [slice(0, J // 2), slice(J // 2, J)]
        entries = [list1[:, 0 : J // 32], list1[:, J // 32 : J // 16]]
        xgs_first = sb("xgs_first", [P, J // 2], U8)
        xg_first = sb("xg_first", [P, J // 2], U16)
        nc.vector.tensor_copy(xg_first[:], xt_sb[:].indirect(entries[0]))
        nc.vector.tensor_copy(xgs_first[:], xs_plane[:].indirect(entries[0]))

        w_dealt = sb("w_dealt", [P, PACK, P], U32)
        w_by_slice = w_raw[:].rearrange("p (m t) -> p t m", t=PACK)
        nc.scalar.copy(w_dealt[:, 0, :], w_by_slice[:, 0, :])
        nc.scalar.copy(w_dealt[:, 1:, :], w_by_slice[:, 1:, :])

        ws_by_slice = ws_raw[:].rearrange("p h (m t) -> p h t m", t=PACK)
        ws_upper = sb("ws_upper", [P, 2, P], U8)
        ws01 = sb("ws01", [P, 2, P], U8)
        nc.vector.tensor_copy(ws_upper[:], ws_by_slice[:, 1, 0:2, :])
        nc.vector.tensor_copy(ws01[:], ws_by_slice[:, 0, 0:2, :])
        nc.vector.tensor_copy(ws01[64:128].rearrange("p t m -> p (t m)").bitcast(I32),
                              ws_upper[0:64].rearrange("p t m -> p (t m)").bitcast(I32))
        xg_second = sb("xg_second", [P, J // 2], U16, tag="ws_upper")
        nc.vector.tensor_copy(xg_second[:], xt_sb[:].indirect(entries[1]))
        xgs_second = sb("xgs_second", [P, J // 2], U8, tag="xt_sb")
        nc.vector.tensor_copy(xgs_second[:], xs_plane[:].indirect(entries[1]))
        xg_words = [xg_first, xg_second]
        xg_scales = [xgs_first, xgs_second]

        def slot_product(dst, words, fmt, plane, g):
            nc.tensor.matmul_mx(dst, lhsT=words.bitcast(fmt), lhsT_scale=plane, rhs=xg_words[g][:].bitcast(E2M1),
                                rhs_scale=xg_scales[g][:], start=True, stop=True)

        def first_results(t, plane, groups, bank):
            a_ps = psum.tile([P, len(groups), J // 2], F32, name="a_ps%d" % bank, tag="bank%d" % bank)
            for i, g in enumerate(groups):
                slot_product(a_ps[:, i, :], w_dealt[:, t, :], E4M3, plane, g)
            a_sb = sb("a_sb%d" % bank, [P, len(groups) * J // 2], F32)
            copy = nc.scalar.copy if bank == 0 else nc.vector.tensor_copy
            copy(a_sb[:], a_ps[:].rearrange("p g j -> p (g j)"))
            columns = slice(groups[0] * J // 32, (groups[-1] + 1) * J // 32)
            nc.scalar.activation(pa[t][:].indirect(list2[:, columns]), a_sb[:], COPY)

        for g in range(2):
            for t in range(2):
                first_results(t, ws01[:, t, :], [g], 2 * g + t)
        ws23 = sb("ws23", [P, 2, 2 * P], U8, tag="xs_plane")
        nc.vector.tensor_copy(ws23[:].rearrange("p h (t m) -> p h t m", t=2), ws_by_slice[:, :, 2:4, :])
        nc.vector.tensor_copy(ws23[64:128, 0, :].bitcast(I32), ws23[0:64, 1, :].bitcast(I32))
        first_results(2, ws23[:, 0, 0:P], [0, 1], 4)
        first_results(3, ws23[:, 0, P : 2 * P], [0, 1], 5)

        w2_dealt = sb("w2_dealt", [P, PACK, P], U32, tag="ws01")
        w2s_dealt = sb("w2s_dealt", [P, PACK, P], U8, tag="ws_raw")
        nc.vector.tensor_copy(w2_dealt[:].rearrange("p t m -> p m t"), w2_raw[:].rearrange("p (m t) -> p m t", t=PACK))
        nc.vector.tensor_copy(w2s_dealt[:], w2s_raw[:].rearrange("p (m t) -> p t m", t=PACK))
        b_ps = [psum.tile([P, 2, J], F32, name="b_ps%d" % u, tag="bank%d" % (6 + u)) for u in range(2)]
        for t in range(PACK):
            for g in range(2):
                slot_product(b_ps[t // 2][:, t % 2, halves[g]], w2_dealt[:, t, :], E5M2, w2s_dealt[:, t, :], g)

        h1 = []
        for t in range(PACK):
            picked = sb("picked%d" % t, [P, J], F32, tag="picked")
            nc.vector.tensor_copy(picked[:], pa[t][:].indirect(list3[:]))
            h_t = sb("h1_%d" % t, [P, J], F32)
            nc.vector.tensor_tensor(h_t[:], b_ps[t // 2][:, t % 2, :], picked[:], MAX)
            h1.append(h_t)
        pb = [sb("pb%d" % t, [P, C], F32, tag=tag) for t, tag in enumerate(("w2_raw", "xgs_first", "xg_first", "ws_upper"))]
        for t in range(PACK):
            nc.vector.memset(pb[t][:], 0.0)
        for t in range(PACK):
            nc.scalar.activation(pb[t][:].indirect(list4[:]), h1[t][:], COPY)

        hid = [sb("hid%d" % u, [P, WIDTH, PACK], BF16) for u in range(CHUNKS)]
        cols = [slice(u * WIDTH, (u + 1) * WIDTH) for u in range(CHUNKS)]
        sums = sb("sums", [P, CHUNKS, PACK, WIDTH], BF16, tag="picked")

        def by_chunk(board):
            return board[:].rearrange("p (u c) -> p u c", u=CHUNKS)

        def weave(copy, u, pair):
            copy(hid[u][:, :, 2 * pair : 2 * pair + 2], sums[:, u, 2 * pair : 2 * pair + 2, :].rearrange("p e c -> p c e"))

        for t in range(2):
            nc.vector.tensor_tensor(sums[:, :, t, :], by_chunk(pa[t]), by_chunk(pb[t]), ADD)
        for u in range(CHUNKS):
            weave(nc.vector.tensor_copy, u, 0)
        nc.vector.tensor_tensor(sums[:, :, 2, :], by_chunk(pa[2]), by_chunk(pb[2]), ADD)

        codes = [sb("codes%d" % u, [P, WIDTH], U32) for u in range(CHUNKS)]
        scales = [sb("scales%d" % u, [P, WIDTH], U8) for u in range(CHUNKS)]

        def add_last(u):
            nc.vector.tensor_tensor(sums[:, u, 3, :], pa[3][:, cols[u]], pb[3][:, cols[u]], ADD)

        def quantise(u):
            nc.vector.quantize_mx(codes[u][:].bitcast(E5M2), scales[u][:], hid[u][:].rearrange("p c t -> p (c t)"))

        add_last(0)
        for u in (1, 3):
            add_last(u)
            weave(nc.scalar.copy, u, 1)
        weave(nc.vector.tensor_copy, 0, 1)
        add_last(2)
        quantise(0)
        weave(nc.vector.tensor_copy, 2, 1)
        for u in range(1, CHUNKS):
            quantise(u)

        def out_product(dst, u, n):
            nc.tensor.matmul_mx(dst, lhsT=wb_sb[:, 2 * P * n : 2 * P * (n + 1)].bitcast(E2M1),
                                lhsT_scale=wbs_plane[:, P * n : P * (n + 1)],
                                rhs=codes[u][:].bitcast(E5M2), rhs_scale=scales[u][:], start=True, stop=True)

        copies = (nc.scalar.copy, nc.vector.tensor_copy)
        for u in range(CHUNKS - 1):
            out_ps = psum.tile([P, 2, WIDTH], F32, name="out_ps%d" % u, tag="bank%d" % u)
            for n in range(2):
                out_product(out_ps[:, n, :], u, n)
            out_sb = sb("out_sb%d" % u, [P, 2, WIDTH], F32)
            copies[u % 2](out_sb[:], out_ps[:])
            nc.sync.dma_start(out[:, cols[u]].rearrange("(n p) c -> p n c", p=P), out_sb[:])
        last = CHUNKS - 1
        for n, queue in enumerate((nc.sync, nc.scalar)):
            last_ps = psum.tile([P, WIDTH], F32, name="last_ps%d" % n, tag="bank%d" % (last + n))
            out_product(last_ps[:], last, n)
            last_sb = sb("last_sb%d" % n, [P, WIDTH], F32)
            copies[1 - n](last_sb[:], last_ps[:])
            queue.dma_start(out[P * n : P * (n + 1), cols[last]], last_sb[:])
